import numpy as np
CORES = [3,11,19,27,35,43,51,59,131,259,387]
N = 11
ROOT = 10
def setup_inputs(rng):
    return {"x": rng.standard_normal((N, 128, 1), dtype=np.float32)}
def reference(x):
    return {"y": np.broadcast_to(x[ROOT], x.shape)}

@@ -1,0 +1,44 @@
+from concourse.bass import DstId, RemoteDMATransfer
+
+SCRATCH = {
+    "land": ("dram", [128, 1], "float32"),
+}
+SEMAPHORES = ["loaded", "sent", "arrived", "stored"]
+
+ROOT = 387
+RELAY = 259
+FAR = 131
+HOST0 = [3, 11, 19, 27, 35, 43, 51, 59]
+
+
+def rank_program(g, core, T, topo):
+    rank = T.rank_of(core)
+    if rank is None:
+        return
+    s = T.sem
+
+    if core == ROOT:
+        g.sync.dma_start(T.land[:], T.x[:]).then_inc(s.loaded, 16)
+        g.wait_ge(s.loaded, 16)
+        rid, pid = topo.addr(RELAY, core)
+        g.remote_dma(T.land[:], T.land[:], s.arrived, s.sent, pid, rid, 0x01)
+        transfers = []
+        for e, d in enumerate(HOST0):
+            rid, pid = topo.addr(d, core)
+            transfers.append(RemoteDMATransfer(dst_ids=[DstId(rid=rid, pnc=pid)], dma_engine_mask=1 << e,
+                                               remote_sem=s.arrived, src=T.land[:], dst=T.land[:]))
+        g.remote_dma_fused(transfers, local_sem=s.sent)
+        g.sync.wait_ge(s.sent, 9)
+        g.sync.dma_start(T.y[:], T.x[:]).then_inc(s.stored, 16)
+        g.sync.wait_ge(s.stored, 16)
+        return
+
+    if core == RELAY:
+        g.wait_ge(s.arrived, 1)
+        rid, pid = topo.addr(FAR, core)
+        g.remote_dma(T.land[:], T.land[:], s.arrived, s.sent, pid, rid, 0x01)
+    g.sync.wait_ge(s.arrived, 1)
+    g.sync.dma_start(T.y[:], T.land[:]).then_inc(s.stored, 16)
+    g.sync.wait_ge(s.stored, 16)
+    if core == RELAY:
+        g.wait_ge(s.sent, 1)

@@ -20,15 +20,17 @@ def rank_program(g, core, T, topo):
     if core == ROOT:
         g.sync.dma_start(T.land[:], T.x[:]).then_inc(s.loaded, 16)
         g.wait_ge(s.loaded, 16)
-        rid, pid = topo.addr(RELAY, core)
-        g.remote_dma(T.land[:], T.land[:], s.arrived, s.sent, pid, rid, 0x01)
+        groups = [[RELAY]] + [[d] for d in HOST0[1:7]] + [[HOST0[7], HOST0[0]]]
         transfers = []
-        for e, d in enumerate(HOST0):
-            rid, pid = topo.addr(d, core)
-            transfers.append(RemoteDMATransfer(dst_ids=[DstId(rid=rid, pnc=pid)], dma_engine_mask=1 << e,
-                                               remote_sem=s.arrived, src=T.land[:], dst=T.land[:]))
+        for e, ds in enumerate(groups):
+            ids = []
+            for d in ds:
+                rid, pid = topo.addr(d, core)
+                ids.append(DstId(rid=rid, pnc=pid))
+            transfers.append(RemoteDMATransfer(dst_ids=ids, dma_engine_mask=1 << e, remote_sem=s.arrived,
+                                               srcs=[T.land[:]], dsts=[T.land[:] for d in ds]))
         g.remote_dma_fused(transfers, local_sem=s.sent)
-        g.sync.wait_ge(s.sent, 9)
+        g.sync.wait_ge(s.sent, 8)
         g.sync.dma_start(T.y[:], T.x[:]).then_inc(s.stored, 16)
         g.sync.wait_ge(s.stored, 16)
         return
@@ -37,8 +39,8 @@ def rank_program(g, core, T, topo):
         g.wait_ge(s.arrived, 1)
         rid, pid = topo.addr(FAR, core)
         g.remote_dma(T.land[:], T.land[:], s.arrived, s.sent, pid, rid, 0x01)
-    g.sync.wait_ge(s.arrived, 1)
+        g.sync.wait_ge(s.sent, 1)
+    else:
+        g.sync.wait_ge(s.arrived, 1)
     g.sync.dma_start(T.y[:], T.land[:]).then_inc(s.stored, 16)
     g.sync.wait_ge(s.stored, 16)
-    if core == RELAY:
-        g.wait_ge(s.sent, 1)

from concourse.bass import DstId, RemoteDMATransfer

SCRATCH = {
    "land": ("dram", [128, 1], "float32"),
}
SEMAPHORES = ["loaded", "sent", "arrived", "stored"]

ROOT = 387
RELAY = 259
FAR = 131
HOST0 = [3, 11, 19, 27, 35, 43, 51, 59]


def rank_program(g, core, T, topo):
    rank = T.rank_of(core)
    if rank is None:
        return
    s = T.sem

    if core == ROOT:
        g.sync.dma_start(T.land[:], T.x[:]).then_inc(s.loaded, 16)
        g.wait_ge(s.loaded, 16)
        groups = [[RELAY]] + [[d] for d in HOST0[1:7]] + [[HOST0[7], HOST0[0]]]
        transfers = []
        for e, ds in enumerate(groups):
            ids = []
            for d in ds:
                rid, pid = topo.addr(d, core)
                ids.append(DstId(rid=rid, pnc=pid))
            transfers.append(RemoteDMATransfer(dst_ids=ids, dma_engine_mask=1 << e, remote_sem=s.arrived,
                                               srcs=[T.land[:]], dsts=[T.land[:] for d in ds]))
        g.remote_dma_fused(transfers, local_sem=s.sent)
        g.sync.wait_ge(s.sent, 8)
        g.sync.dma_start(T.y[:], T.x[:]).then_inc(s.stored, 16)
        g.sync.wait_ge(s.stored, 16)
        return

    if core == RELAY:
        g.wait_ge(s.arrived, 1)
        rid, pid = topo.addr(FAR, core)
        g.remote_dma(T.land[:], T.land[:], s.arrived, s.sent, pid, rid, 0x01)
        g.sync.wait_ge(s.sent, 1)
    else:
        g.sync.wait_ge(s.arrived, 1)
    g.sync.dma_start(T.y[:], T.land[:]).then_inc(s.stored, 16)
    g.sync.wait_ge(s.stored, 16)
